import numpy as np
import ml_dtypes


def mxq(x, axis, fmt="e4m3"):
    dtype, down = {"e4m3": (ml_dtypes.float8_e4m3fn, 7), "e5m2": (ml_dtypes.float8_e5m2, 14)}[fmt]
    v = np.moveaxis(np.asarray(x, np.float32).astype(ml_dtypes.bfloat16).astype(np.float64), axis, -1)
    blocks = v.reshape(v.shape[:-1] + (-1, 32))
    amax = np.abs(blocks).max(-1, keepdims=True)
    byte = np.maximum(np.where(amax > 0, np.frexp(amax)[1] - 1 + 127, 0) - down, 1)
    scale = np.exp2(byte - 127.0)
    codes = (blocks / scale).astype(np.float32).astype(dtype).astype(np.float64)
    return np.moveaxis((codes * scale).reshape(v.shape), -1, axis)


WIDE = False


def mx_kscale(k):
    if not WIDE:
        return np.ones(k)
    levels = np.array([10, -10, 5, -5, 0])
    if k % 512:
        return np.exp2(np.random.permutation(np.resize(levels, k // 32))).repeat(32)
    a = np.empty((k // 512, 16))
    for p in range(k // 512):
        a[p, :8] = np.random.permutation(np.resize(levels, 8))
        for g in range(8):
            far = levels[np.abs(levels - a[p, g]) >= 10]
            a[p, g + 8] = far[np.random.randint(len(far))]
    return np.exp2(a.ravel()).repeat(32)


def f64(x):
    return np.asarray(x).astype(np.float64)


def striped(idx):
    return np.tile(np.asarray(idx).reshape(-1, 16).T, (8, 1)).astype(np.uint16)


def unstriped(offs):
    return offs[:16].T.reshape(-1).astype(np.int64)


E2M1 = np.array([0.0, 0.5, 1.0, 1.5, 2.0, 3.0, 4.0, 6.0, -0.0, -0.5, -1.0, -1.5, -2.0, -3.0, -4.0, -6.0])


def pack_weight(w, fmt):
    k, n = w.shape
    w = f64(np.asarray(w, np.float32).astype(ml_dtypes.bfloat16)).reshape(k // 32, 32, n)
    amax = np.abs(w).max(1)
    if fmt == "e4m3":
        byte = np.frexp(amax)[1] - 1 + 127 - 7
    else:
        mant, ex = np.frexp(amax / 6.0)
        byte = np.where(mant > 0.5, ex, ex - 1) + 127
    byte = np.clip(np.where(amax > 0, byte, 1), 1, 254)
    scaled = (w * np.exp2(127.0 - byte)[:, None, :]).reshape(k, n).astype(np.float32)
    by_word = np.ascontiguousarray(scaled.reshape(k // 512, 128, 4, n).transpose(0, 1, 3, 2))
    if fmt == "e4m3":
        words = by_word.astype(ml_dtypes.float8_e4m3fn).view(np.uint8)
    else:
        c = by_word.astype(ml_dtypes.float4_e2m1fn).view(np.uint8) & 0xF
        words = (c[..., 0::2] | (c[..., 1::2] << 4)).reshape(k // 512, 128, 2 * n)
    return np.ascontiguousarray(words), np.ascontiguousarray(byte.astype(np.uint8).reshape(k // 512, 16, n))


def unpack_weight(words, scales, fmt):
    g, _, n = scales.shape
    words = np.ascontiguousarray(words).reshape(g, 128, n, -1)
    if fmt == "e4m3":
        vals = words.view(ml_dtypes.float8_e4m3fn).astype(np.float64)
    else:
        nib = np.empty((g, 128, n, 4), np.uint8)
        nib[..., 0::2] = words & 0xF
        nib[..., 1::2] = words >> 4
        vals = E2M1[nib]
    vals = vals * np.repeat(np.exp2(scales.astype(np.float64) - 127.0), 8, axis=1)[..., None]
    return vals.transpose(0, 1, 3, 2).reshape(g * 512, n)


D, E, T, I, U, Q = 512, 512, 2048, 256, 1024, 512


def setup_inputs():
    n = np.random.standard_normal
    idx = np.random.permutation(T)[:I]
    idx2 = np.random.permutation(U)[:I]
    fd = mx_kscale(D)
    fq = mx_kscale(Q)
    keysp = pack_weight(n((D, T)) / fd[:, None], "e4m3")
    return {
        "query": (n((D, Q)) * 0.5 / np.sqrt(D) * fd[:, None]).astype(np.float32),
        "keys_words": keysp[0],
        "keys_scales": keysp[1],
        "qs": (np.random.uniform(8.0, 32.0, (Q, 1)) * fq[:, None]).astype(np.float32),
        "grows": (n((Q, E)) / fq[:, None]).astype(np.float32),
        "old": (n((E, U)) * 4.0).astype(np.float32),
        "fade": (np.random.uniform(0.5, 1.0, (1, U))).astype(np.float32),
        "offs": striped(idx),
        "offs2": striped(idx2),
    }


def reference(query, keys_words, keys_scales, qs, grows, old, fade, offs, offs2):
    idx = unstriped(offs)
    idx2 = unstriped(offs2)
    keysu = unpack_weight(keys_words, keys_scales, "e4m3")
    queryq = mxq(f64(query), 0, "e4m3")
    keysidxg = keysu[:, idx]
    a = queryq.T @ keysidxg
    p = np.exp(a - np.max(a, axis=1, keepdims=True))
    w = p * f64(qs) / np.sum(p, axis=1, keepdims=True)
    growsq = mxq(f64(grows), 0, "e4m3")
    wq = mxq(w, 0, "e4m3")
    dv = growsq.T @ wq
    vf = np.zeros((E, U))
    vf[:, idx2] = dv
    y = f64(old) * f64(fade) + vf
    return y

@@ -1,0 +1,260 @@
+from contextlib import ExitStack
+
+import concourse.mybir as mybir
+from concourse.masks import make_identity
+
+D, E, T, I, U, Q = 512, 512, 2048, 256, 1024, 512
+FLOPS = 2 * D * Q * I + 2 * Q * E * I
+
+F32 = mybir.dt.float32
+BF16 = mybir.dt.bfloat16
+I32 = mybir.dt.int32
+U32 = mybir.dt.uint32
+U16 = mybir.dt.uint16
+U8 = mybir.dt.uint8
+FP8X4 = mybir.dt.float8_e4m3fn_x4
+ALU = mybir.AluOpType
+ACT = mybir.ActivationFunctionType
+
+P = 128
+PACK = 4
+E_TILES = E // P
+HALF = U // 2
+HALF_BLOCKS = HALF // P
+QUERY_SPLIT = 96
+RUN = U // P
+WINDOWS = 3
+
+
+def tile_attend_gvaluestore_kernel(tc, query, keys_words, keys_scales, qs, grows, old, fade, offs, offs2, out):
+    nc = tc.nc
+    with ExitStack() as ctx:
+        sb = ctx.enter_context(tc.tile_pool(name="sb", bufs=1))
+        ps = ctx.enter_context(tc.psum_pool(name="ps", bufs=1))
+
+        def bank(n, shape, name):
+            return ps.tile(shape, F32, name=name, tag="bank%d" % n)
+
+        scale_pool = sb.tile([P, T], U8, name="scale_pool")
+        nc.vector.memset(scale_pool[:].bitcast(I32), 0)
+        slots = sb.tile([P, I // 16], U16, name="slots")
+        nc.sync.dma_start(slots[:], offs)
+        places = sb.tile([P, I // 16], U16, name="places")
+        nc.sync.dma_start(places[:], offs2)
+        q_raw = sb.tile([P, PACK, Q], F32, name="q_raw")
+        nc.sync.dma_start(out=q_raw[:], in_=query.rearrange("(p j) q -> p j q", j=PACK))
+        row_scale = sb.tile([P, PACK], F32, name="row_scale")
+        nc.sync.dma_start(out=row_scale[:], in_=qs.rearrange("(p r) o -> p (r o)", r=PACK))
+        fade_runs = sb.tile([P, RUN], F32, name="fade_runs")
+        nc.sync.dma_start(out=fade_runs[:], in_=fade.rearrange("o (p c) -> (o p) c", c=RUN))
+        for quad in range(4):
+            nc.sync.dma_start(
+                out=scale_pool[32 * quad : 32 * quad + 4, :].bitcast(I32),
+                in_=keys_scales[0, 4 * quad : 4 * quad + 4, :].bitcast(I32),
+            )
+        key_pool = sb.tile([P, T], U32, name="key_pool")
+        nc.sync.dma_start(out=key_pool[:].bitcast(I32), in_=keys_words[0].rearrange("p t r -> p (t r)").bitcast(I32))
+        g_raw = sb.tile([P, PACK, E], F32, name="g_raw")
+        nc.sync.dma_start(out=g_raw[:], in_=grows.rearrange("(p j) e -> p j e", j=PACK))
+        old_tiles = old.rearrange("(m p) u -> p m u", p=P)
+        old_hi = sb.tile([P, E_TILES, HALF], F32, name="old_hi")
+        nc.sync.dma_start(out=old_hi[:], in_=old_tiles[:, :, HALF:U])
+        old_lo = []
+        for pair in range(E_TILES // 2):
+            t = sb.tile([P, 2, HALF], F32, name="old_lo%d" % pair)
+            nc.sync.dma_start(out=t[:], in_=old_tiles[:, 2 * pair : 2 * pair + 2, 0:HALF])
+            old_lo.append(t)
+
+        ident = sb.tile([P, P], F32, name="ident")
+        make_identity(nc, ident[:])
+        windows = []
+        for n in range(WINDOWS):
+            t = sb.tile([P, U], F32, name="window%d" % n)
+            (nc.gpsimd if n == WINDOWS - 1 else nc.vector).memset(t[:], 0.0)
+            windows.append(t)
+        stores = [windows[m % WINDOWS] for m in range(E_TILES)]
+
+        k_scales = sb.tile([P, I], U8, name="k_scales", align_bytes=64)
+        nc.vector.tensor_copy(k_scales[:], scale_pool[:].indirect(slots[:]))
+
+        fade_rows = sb.tile([P, U], F32, name="fade_rows")
+        fade_by_run = fade_rows[:].rearrange("p (n c) -> p n c", c=RUN)
+        for h in range(2):
+            spread = bank(6 + h, [P, 4, P], "spread%d" % h)
+            for c in range(4):
+                col = 4 * h + c
+                nc.tensor.transpose(spread[:, c, :], fade_runs[:, col : col + 1].to_broadcast([P, P]), ident[:])
+            nc.scalar.copy(fade_by_run[:, :, 4 * h : 4 * h + 4], spread[:].rearrange("p c n -> p n c"))
+        fade_ps = bank(5, [P, HALF_BLOCKS, P], "fade_ps")
+        for b in range(HALF_BLOCKS):
+            nc.tensor.transpose(fade_ps[:, b, :], fade_rows[:, HALF + b * P : HALF + (b + 1) * P], ident[:])
+        fade_cols = sb.tile([P, HALF_BLOCKS], F32, name="fade_cols")
+        nc.scalar.copy(fade_cols[:], fade_ps[:, :, 0])
+
+        q_bf = sb.tile([P, Q * PACK], BF16, name="q_bf", align_bytes=64)
+        q_dst = q_bf[:].rearrange("p (r s j) -> p s j r", r=PACK, j=PACK)
+        q_src = q_raw[:].rearrange("p j (s r) -> p s j r", r=PACK)
+        nc.vector.tensor_copy(q_dst[:, 0:QUERY_SPLIT], q_src[:, 0:QUERY_SPLIT])
+        nc.scalar.copy(q_dst[:, QUERY_SPLIT:P], q_src[:, QUERY_SPLIT:P])
+        q_codes = sb.tile([P, Q], U32, name="q_codes", align_bytes=64)
+        q_scales = sb.tile([P, Q], U8, name="q_scales", align_bytes=64)
+        nc.vector.quantize_mx(out=q_codes[:].bitcast(FP8X4), scales=q_scales[:], in_=q_bf[:])
+
+        k_codes = sb.tile([P, I], U32, name="k_codes", align_bytes=64)
+        nc.vector.tensor_copy(k_codes[:], key_pool[:].indirect(slots[:]))
+
+        neg_max = sb.tile([P, PACK], F32, name="neg_max", tag="relay_a", align_bytes=64)
+        row_sum = sb.tile([P, PACK], F32, name="row_sum", tag="relay_b", align_bytes=64)
+        inv_sum = sb.tile([P, PACK], F32, name="inv_sum")
+        probs = sb.tile([P, PACK, I], F32, name="probs")
+        w_bf = sb.tile([P, I * PACK], BF16, name="w_bf", align_bytes=64)
+        w_places = w_bf[:].rearrange("p (i r) -> p r i", r=PACK)
+        for r in range(PACK):
+            scores = bank(r, [P, I], "scores%d" % r)
+            cols = slice(r * P, (r + 1) * P)
+            nc.tensor.matmul_mx(
+                out=scores[:],
+                lhsT=q_codes[:, cols].bitcast(FP8X4),
+                lhsT_scale=q_scales[:, cols],
+                rhs=k_codes[:].bitcast(FP8X4),
+                rhs_scale=k_scales[:],
+                start=True,
+                stop=True,
+            )
+            nc.vector.tensor_reduce(out=neg_max[:, r : r + 1], in_=scores[:], axis=mybir.AxisListType.X, op=ALU.max, negate=True)
+            nc.scalar.activation(
+                out=probs[:, r, :], in_=scores[:], func=ACT.Exp, bias=neg_max[:, r : r + 1], accum_out=row_sum[:, r : r + 1]
+            )
+
+        def invert(lo, hi):
+            nc.vector.reciprocal(inv_sum[:, lo:hi], row_sum[:, lo:hi])
+
+        def weigh(r):
+            nc.vector.tensor_scalar(
+                out=w_places[:, r, :],
+                in0=probs[:, r, :],
+                scalar1=inv_sum[:, r : r + 1],
+                scalar2=row_scale[:, r : r + 1],
+                op0=ALU.mult,
+                op1=ALU.mult,
+            )
+
+        invert(0, 1)
+        invert(1, 2)
+        weigh(0)
+        invert(2, 3)
+        weigh(1)
+        invert(3, 4)
+        weigh(2)
+        weigh(3)
+
+        g_first = sb.tile([P, P * PACK], BF16, name="g_first", tag="relay_a", align_bytes=64)
+        g_rest = sb.tile([P, (E - P) * PACK], BF16, name="g_rest", tag="relay_b", align_bytes=64)
+
+        def g_bf(lo, hi):
+            return g_first[:] if lo == 0 else g_rest[:, (lo - 1) * P * PACK : (hi - 1) * P * PACK]
+
+        g_codes = sb.tile([P, E], U32, name="g_codes", align_bytes=64)
+        g_scales = sb.tile([P, E], U8, name="g_scales", align_bytes=64)
+
+        def round_g(m, copy):
+            copy(
+                g_bf(m, m + 1).rearrange("p (c n j) -> p c j n", n=4, j=PACK),
+                g_raw[:, :, m * P : (m + 1) * P].rearrange("p j (c n) -> p c j n", n=4),
+            )
+
+        def quantize_g(lo, hi):
+            cols = slice(lo * P, hi * P)
+            nc.vector.quantize_mx(
+                out=g_codes[:, cols].bitcast(FP8X4), scales=g_scales[:, cols], in_=g_bf(lo, hi)
+            )
+
+        for m in range(E_TILES - 1):
+            round_g(m, nc.scalar.copy)
+        quantize_g(0, 1)
+        w_codes = sb.tile([P, I], U32, name="w_codes", align_bytes=64)
+        w_scales = sb.tile([P, I], U8, name="w_scales", align_bytes=64)
+        nc.vector.quantize_mx(out=w_codes[:].bitcast(FP8X4), scales=w_scales[:], in_=w_bf[:])
+        round_g(E_TILES - 1, nc.vector.tensor_copy)
+        quantize_g(1, 2)
+        quantize_g(2, 4)
+
+        dv = []
+
+        def value_gradient(m):
+            acc = bank(6 + m % 2, [P, I], "dv_ps%d" % m)
+            cols = slice(m * P, (m + 1) * P)
+            nc.tensor.matmul_mx(
+                out=acc[:],
+                lhsT=g_codes[:, cols].bitcast(FP8X4),
+                lhsT_scale=g_scales[:, cols],
+                rhs=w_codes[:].bitcast(FP8X4),
+                rhs_scale=w_scales[:],
+                start=True,
+                stop=True,
+            )
+            t = sb.tile([P, I], F32, name="dv%d" % m)
+            (nc.vector.tensor_copy if m == 0 else nc.scalar.copy)(t[:], acc[:])
+            dv.append(t)
+
+        faded_t = []
+
+        def fade_turned(b):
+            turned = bank(b, [P, E_TILES, P], "turned%d" % b)
+            for m in range(E_TILES):
+                nc.tensor.transpose(turned[:, m, :], old_hi[:, m, b * P : (b + 1) * P], ident[:])
+            t = sb.tile([P, E], F32, name="faded_t%d" % b)
+            nc.scalar.activation(
+                out=t[:], in_=turned[:].rearrange("p m e -> p (m e)"), func=ACT.Copy, scale=fade_cols[:, b : b + 1]
+            )
+            faded_t.append(t)
+
+        value_gradient(0)
+        value_gradient(1)
+        fade_turned(0)
+        fade_turned(1)
+        value_gradient(2)
+        fade_turned(2)
+        fade_turned(3)
+        value_gradient(3)
+        faded_hi = []
+        for m in range(E_TILES):
+            back = bank((4 + m) % 6, [P, HALF_BLOCKS, P], "faded_hi%d" % m)
+            for b in range(HALF_BLOCKS):
+                nc.tensor.transpose(back[:, b, :], faded_t[b][:, m * P : (m + 1) * P], ident[:])
+            faded_hi.append(back)
+
+        faded_lo = sb.tile([P, E_TILES, HALF], F32, name="faded_lo", tag="relay_b", align_bytes=64)
+        fade_lo = fade_rows[:, 0:HALF].rearrange("p (o u) -> p o u", o=1).to_broadcast([P, 2, HALF])
+
+        def fade_low(pair):
+            nc.gpsimd.tensor_tensor(out=faded_lo[:, 2 * pair : 2 * pair + 2, :], in0=old_lo[pair][:], in1=fade_lo, op=ALU.mult)
+
+        def finish_low(m, engine, lo, hi):
+            y = sb.tile([P, hi - lo], F32, name="y_lo%d_%d" % (m, lo))
+            engine.tensor_tensor(out=y[:], in0=faded_lo[:, m, lo:hi], in1=stores[m][:, lo:hi], op=ALU.add)
+            nc.sync.dma_start(out=out[m * P : (m + 1) * P, lo:hi], in_=y[:])
+
+        def finish_high(m):
+            y = sb.tile([P, HALF], F32, name="y_hi%d" % m)
+            nc.vector.tensor_tensor(
+                out=y[:], in0=faded_hi[m][:].rearrange("p b c -> p (b c)"), in1=stores[m][:, HALF:U], op=ALU.add
+            )
+            nc.scalar.dma_start(out=out[m * P : (m + 1) * P, HALF:U], in_=y[:])
+
+        def scatter(m):
+            nc.vector.tensor_copy(stores[m][:].indirect(places[:]), dv[m][:])
+
+        for m in range(WINDOWS):
+            scatter(m)
+        fade_low(0)
+        finish_low(0, nc.gpsimd, 0, HALF)
+        finish_low(1, nc.gpsimd, 0, HALF)
+        fade_low(1)
+        finish_low(2, nc.gpsimd, 0, HALF)
+        finish_high(0)
+        scatter(3)
+        finish_low(3, nc.gpsimd, 0, HALF // 2)
+        for m in range(1, E_TILES):
+            finish_high(m)
+        finish_low(3, nc.vector, HALF // 2, HALF)

@@ -47,15 +47,17 @@ def tile_attend_gvaluestore_kernel(tc, query, keys_words, keys_scales, qs, grows
         nc.sync.dma_start(out=row_scale[:], in_=qs.rearrange("(p r) o -> p (r o)", r=PACK))
         fade_runs = sb.tile([P, RUN], F32, name="fade_runs")
         nc.sync.dma_start(out=fade_runs[:], in_=fade.rearrange("o (p c) -> (o p) c", c=RUN))
-        for quad in range(4):
+        for row in range(4):
             nc.sync.dma_start(
-                out=scale_pool[32 * quad : 32 * quad + 4, :].bitcast(I32),
-                in_=keys_scales[0, 4 * quad : 4 * quad + 4, :].bitcast(I32),
+                out=scale_pool[row:P:32, :].bitcast(I32), in_=keys_scales[0, row:16:4, :].bitcast(I32)
             )
         key_pool = sb.tile([P, T], U32, name="key_pool")
         nc.sync.dma_start(out=key_pool[:].bitcast(I32), in_=keys_words[0].rearrange("p t r -> p (t r)").bitcast(I32))
-        g_raw = sb.tile([P, PACK, E], F32, name="g_raw")
-        nc.sync.dma_start(out=g_raw[:], in_=grows.rearrange("(p j) e -> p j e", j=PACK))
+        g_rows = grows.rearrange("(p j) e -> p j e", j=PACK)
+        g_raw_hi = sb.tile([P, PACK, E // 2], F32, name="g_raw_hi")
+        nc.sync.dma_start(out=g_raw_hi[:], in_=g_rows[:, :, E // 2 : E])
+        g_raw_lo = sb.tile([P, PACK, E // 2], F32, name="g_raw_lo")
+        nc.sync.dma_start(out=g_raw_lo[:], in_=g_rows[:, :, 0 : E // 2])
         old_tiles = old.rearrange("(m p) u -> p m u", p=P)
         old_hi = sb.tile([P, E_TILES, HALF], F32, name="old_hi")
         nc.sync.dma_start(out=old_hi[:], in_=old_tiles[:, :, HALF:U])
@@ -72,7 +74,7 @@ def tile_attend_gvaluestore_kernel(tc, query, keys_words, keys_scales, qs, grows
             t = sb.tile([P, U], F32, name="window%d" % n)
             (nc.gpsimd if n == WINDOWS - 1 else nc.vector).memset(t[:], 0.0)
             windows.append(t)
-        stores = [windows[m % WINDOWS] for m in range(E_TILES)]
+        stores = windows + [windows[1]]
 
         k_scales = sb.tile([P, I], U8, name="k_scales", align_bytes=64)
         nc.vector.tensor_copy(k_scales[:], scale_pool[:].indirect(slots[:]))
@@ -107,8 +109,7 @@ def tile_attend_gvaluestore_kernel(tc, query, keys_words, keys_scales, qs, grows
         row_sum = sb.tile([P, PACK], F32, name="row_sum", tag="relay_b", align_bytes=64)
         inv_sum = sb.tile([P, PACK], F32, name="inv_sum")
         probs = sb.tile([P, PACK, I], F32, name="probs")
-        w_bf = sb.tile([P, I * PACK], BF16, name="w_bf", align_bytes=64)
-        w_places = w_bf[:].rearrange("p (i r) -> p r i", r=PACK)
+        w_planes = sb.tile([P, PACK, I], BF16, name="w_planes")
         for r in range(PACK):
             scores = bank(r, [P, I], "scores%d" % r)
             cols = slice(r * P, (r + 1) * P)
@@ -129,73 +130,91 @@ def tile_attend_gvaluestore_kernel(tc, query, keys_words, keys_scales, qs, grows
         def invert(lo, hi):
             nc.vector.reciprocal(inv_sum[:, lo:hi], row_sum[:, lo:hi])
 
-        def weigh(r):
+        def weigh(r, lo, hi):
             nc.vector.tensor_scalar(
-                out=w_places[:, r, :],
-                in0=probs[:, r, :],
+                out=w_planes[:, r, lo:hi],
+                in0=probs[:, r, lo:hi],
                 scalar1=inv_sum[:, r : r + 1],
                 scalar2=row_scale[:, r : r + 1],
                 op0=ALU.mult,
                 op1=ALU.mult,
             )
 
-        invert(0, 1)
-        invert(1, 2)
-        weigh(0)
-        invert(2, 3)
-        weigh(1)
-        invert(3, 4)
-        weigh(2)
-        weigh(3)
-
-        g_first = sb.tile([P, P * PACK], BF16, name="g_first", tag="relay_a", align_bytes=64)
-        g_rest = sb.tile([P, (E - P) * PACK], BF16, name="g_rest", tag="relay_b", align_bytes=64)
-
-        def g_bf(lo, hi):
-            return g_first[:] if lo == 0 else g_rest[:, (lo - 1) * P * PACK : (hi - 1) * P * PACK]
-
         g_codes = sb.tile([P, E], U32, name="g_codes", align_bytes=64)
         g_scales = sb.tile([P, E], U8, name="g_scales", align_bytes=64)
-
-        def round_g(m, copy):
-            copy(
-                g_bf(m, m + 1).rearrange("p (c n j) -> p c j n", n=4, j=PACK),
-                g_raw[:, :, m * P : (m + 1) * P].rearrange("p j (c n) -> p c j n", n=4),
+        g_late = sb.tile([P, 2 * P * PACK], BF16, name="g_late", align_bytes=64)
+        for n in range(2):
+            nc.gpsimd.tensor_scalar(
+                out=g_late[:, n * P * PACK : (n + 1) * P * PACK].rearrange("p (e j) -> p e j", j=PACK),
+                in0=g_raw_hi[:, :, n * P : (n + 1) * P].rearrange("p j e -> p e j"),
+                scalar1=1.0,
+                scalar2=0.0,
+                op0=ALU.mult,
+                op1=ALU.add,
             )
 
-        def quantize_g(lo, hi):
+        def quantize_g(lo, hi, rounded):
             cols = slice(lo * P, hi * P)
-            nc.vector.quantize_mx(
-                out=g_codes[:, cols].bitcast(FP8X4), scales=g_scales[:, cols], in_=g_bf(lo, hi)
-            )
+            nc.vector.quantize_mx(out=g_codes[:, cols].bitcast(FP8X4), scales=g_scales[:, cols], in_=rounded[:])
 
-        for m in range(E_TILES - 1):
-            round_g(m, nc.scalar.copy)
-        quantize_g(0, 1)
+        invert(0, 2)
+        invert(2, 3)
+        weigh(0, 0, I)
+        weigh(1, 0, I)
+        invert(3, 4)
+        weigh(2, 0, I)
+        weigh(3, 0, P)
+
+        g_early = []
+        for m, tag in enumerate(("relay_a", "relay_b")):
+            t = sb.tile([P, P * PACK], BF16, name="g_early%d" % m, tag=tag, align_bytes=64)
+            nc.scalar.copy(
+                t[:].rearrange("p (c n j) -> p c j n", n=4, j=PACK),
+                g_raw_lo[:, :, m * P : (m + 1) * P].rearrange("p j (c n) -> p c j n", n=4),
+            )
+            g_early.append(t)
+
+        w_bf = sb.tile([P, I * PACK], BF16, name="w_bf", tag="relay_c", align_bytes=64)
         w_codes = sb.tile([P, I], U32, name="w_codes", align_bytes=64)
         w_scales = sb.tile([P, I], U8, name="w_scales", align_bytes=64)
-        nc.vector.quantize_mx(out=w_codes[:].bitcast(FP8X4), scales=w_scales[:], in_=w_bf[:])
-        round_g(E_TILES - 1, nc.vector.tensor_copy)
-        quantize_g(1, 2)
-        quantize_g(2, 4)
 
-        dv = []
+        def weave(lo, hi, copy):
+            copy(
+                w_bf[:, lo * PACK : hi * PACK].rearrange("p (c n r) -> p c r n", n=4, r=PACK),
+                w_planes[:, :, lo:hi].rearrange("p r (c n) -> p c r n", n=4),
+            )
 
-        def value_gradient(m):
-            acc = bank(6 + m % 2, [P, I], "dv_ps%d" % m)
+        def quantize_w(lo, hi):
+            nc.vector.quantize_mx(
+                out=w_codes[:, lo:hi].bitcast(FP8X4), scales=w_scales[:, lo:hi], in_=w_bf[:, lo * PACK : hi * PACK]
+            )
+
+        quantize_g(0, 1, g_early[0])
+        weave(0, P, nc.vector.tensor_copy)
+        weigh(3, P, I)
+        quantize_w(0, P)
+        weave(P, I, nc.scalar.copy)
+        quantize_g(2, 4, g_late)
+        quantize_g(1, 2, g_early[1])
+        quantize_w(P, I)
+
+        dv = {}
+
+        def value_gradient(m, lo, hi, n, copy):
+            acc = bank(n, [P, hi - lo], "dv_ps%d_%d" % (m, lo))
             cols = slice(m * P, (m + 1) * P)
             nc.tensor.matmul_mx(
                 out=acc[:],
                 lhsT=g_codes[:, cols].bitcast(FP8X4),
                 lhsT_scale=g_scales[:, cols],
-                rhs=w_codes[:].bitcast(FP8X4),
-                rhs_scale=w_scales[:],
+                rhs=w_codes[:, lo:hi].bitcast(FP8X4),
+                rhs_scale=w_scales[:, lo:hi],
                 start=True,
                 stop=True,
             )
-            t = sb.tile([P, I], F32, name="dv%d" % m)
-            (nc.vector.tensor_copy if m == 0 else nc.scalar.copy)(t[:], acc[:])
-            dv.append(t)
+            t = sb.tile([P, hi - lo], F32, name="dv%d_%d" % (m, lo))
+            copy(t[:], acc[:])
+            dv[m, lo] = t
 
         faded_t = []
 
@@ -209,26 +228,32 @@ def tile_attend_gvaluestore_kernel(tc, query, keys_words, keys_scales, qs, grows
             )
             faded_t.append(t)
 
-        value_gradient(0)
-        value_gradient(1)
+        value_gradient(0, 0, P, 6, nc.scalar.copy)
+        value_gradient(1, 0, I, 7, nc.scalar.copy)
+        value_gradient(0, P, I, 6, nc.scalar.copy)
         fade_turned(0)
         fade_turned(1)
-        value_gradient(2)
+        value_gradient(2, 0, I, 7, nc.scalar.copy)
         fade_turned(2)
         fade_turned(3)
-        value_gradient(3)
-        faded_hi = []
-        for m in range(E_TILES):
-            back = bank((4 + m) % 6, [P, HALF_BLOCKS, P], "faded_hi%d" % m)
+        value_gradient(3, 0, I, 6, nc.scalar.copy)
+        faded_hi = {}
+        for n, m in enumerate((0, 2, 1, 3)):
+            back = bank((4 + n) % 6, [P, HALF_BLOCKS, P], "faded_hi%d" % m)
             for b in range(HALF_BLOCKS):
                 nc.tensor.transpose(back[:, b, :], faded_t[b][:, m * P : (m + 1) * P], ident[:])
-            faded_hi.append(back)
+            faded_hi[m] = back
 
-        faded_lo = sb.tile([P, E_TILES, HALF], F32, name="faded_lo", tag="relay_b", align_bytes=64)
-        fade_lo = fade_rows[:, 0:HALF].rearrange("p (o u) -> p o u", o=1).to_broadcast([P, 2, HALF])
+        faded_lo = sb.tile([P, E_TILES, HALF], F32, name="faded_lo", tag="relay_c", align_bytes=64)
+        fade_lo = fade_rows[:, 0:HALF].rearrange("p (o u) -> p o u", o=1)
 
-        def fade_low(pair):
-            nc.gpsimd.tensor_tensor(out=faded_lo[:, 2 * pair : 2 * pair + 2, :], in0=old_lo[pair][:], in1=fade_lo, op=ALU.mult)
+        def fade_low(lo, hi):
+            nc.gpsimd.tensor_tensor(
+                out=faded_lo[:, lo:hi, :],
+                in0=old_lo[lo // 2][:, lo % 2 : lo % 2 + hi - lo, :],
+                in1=fade_lo.to_broadcast([P, hi - lo, HALF]),
+                op=ALU.mult,
+            )
 
         def finish_low(m, engine, lo, hi):
             y = sb.tile([P, hi - lo], F32, name="y_lo%d_%d" % (m, lo))
@@ -242,19 +267,21 @@ def tile_attend_gvaluestore_kernel(tc, query, keys_words, keys_scales, qs, grows
             )
             nc.scalar.dma_start(out=out[m * P : (m + 1) * P, HALF:U], in_=y[:])
 
-        def scatter(m):
-            nc.vector.tensor_copy(stores[m][:].indirect(places[:]), dv[m][:])
+        def scatter(m, lo, hi):
+            nc.vector.tensor_copy(stores[m][:].indirect(places[:, lo // 16 : hi // 16]), dv[m, lo][:])
 
-        for m in range(WINDOWS):
-            scatter(m)
-        fade_low(0)
-        finish_low(0, nc.gpsimd, 0, HALF)
+        scatter(0, 0, P)
+        scatter(1, 0, I)
+        scatter(0, P, I)
+        scatter(2, 0, I)
+        fade_low(0, 2)
+        fade_low(2, 4)
         finish_low(1, nc.gpsimd, 0, HALF)
-        fade_low(1)
+        finish_low(0, nc.gpsimd, 0, HALF)
         finish_low(2, nc.gpsimd, 0, HALF)
-        finish_high(0)
-        scatter(3)
-        finish_low(3, nc.gpsimd, 0, HALF // 2)
-        for m in range(1, E_TILES):
+        for m in (0, 2, 1):
             finish_high(m)
+        scatter(3, 0, I)
+        finish_low(3, nc.gpsimd, 0, HALF // 2)
+        finish_high(3)
         finish_low(3, nc.vector, HALF // 2, HALF)

@@ -21,7 +21,7 @@ PACK = 4
 E_TILES = E // P
 HALF = U // 2
 HALF_BLOCKS = HALF // P
-QUERY_SPLIT = 96
+QUERY_SPLIT = 80
 RUN = U // P
 WINDOWS = 3
 
@@ -53,19 +53,17 @@ def tile_attend_gvaluestore_kernel(tc, query, keys_words, keys_scales, qs, grows
             )
         key_pool = sb.tile([P, T], U32, name="key_pool")
         nc.sync.dma_start(out=key_pool[:].bitcast(I32), in_=keys_words[0].rearrange("p t r -> p (t r)").bitcast(I32))
-        g_rows = grows.rearrange("(p j) e -> p j e", j=PACK)
-        g_raw_hi = sb.tile([P, PACK, E // 2], F32, name="g_raw_hi")
-        nc.sync.dma_start(out=g_raw_hi[:], in_=g_rows[:, :, E // 2 : E])
-        g_raw_lo = sb.tile([P, PACK, E // 2], F32, name="g_raw_lo")
-        nc.sync.dma_start(out=g_raw_lo[:], in_=g_rows[:, :, 0 : E // 2])
         old_tiles = old.rearrange("(m p) u -> p m u", p=P)
+        old_lo0 = sb.tile([P, HALF], F32, name="old_lo0", tag="relay_a", align_bytes=64)
+        nc.sync.dma_start(out=old_lo0[:], in_=old_tiles[:, 0, 0:HALF])
+        old_lo1 = sb.tile([P, HALF], F32, name="old_lo1")
+        nc.sync.dma_start(out=old_lo1[:], in_=old_tiles[:, 1, 0:HALF])
+        g_raw = sb.tile([P, PACK, E], F32, name="g_raw")
+        nc.sync.dma_start(out=g_raw[:], in_=grows.rearrange("(p j) e -> p j e", j=PACK))
         old_hi = sb.tile([P, E_TILES, HALF], F32, name="old_hi")
         nc.sync.dma_start(out=old_hi[:], in_=old_tiles[:, :, HALF:U])
-        old_lo = []
-        for pair in range(E_TILES // 2):
-            t = sb.tile([P, 2, HALF], F32, name="old_lo%d" % pair)
-            nc.sync.dma_start(out=t[:], in_=old_tiles[:, 2 * pair : 2 * pair + 2, 0:HALF])
-            old_lo.append(t)
+        old_lo23 = sb.tile([P, 2, HALF], F32, name="old_lo23", tag="relay_d")
+        nc.sync.dma_start(out=old_lo23[:], in_=old_tiles[:, 2:4, 0:HALF])
 
         ident = sb.tile([P, P], F32, name="ident")
         make_identity(nc, ident[:])
@@ -74,7 +72,7 @@ def tile_attend_gvaluestore_kernel(tc, query, keys_words, keys_scales, qs, grows
             t = sb.tile([P, U], F32, name="window%d" % n)
             (nc.gpsimd if n == WINDOWS - 1 else nc.vector).memset(t[:], 0.0)
             windows.append(t)
-        stores = windows + [windows[1]]
+        stores = windows + [windows[0]]
 
         k_scales = sb.tile([P, I], U8, name="k_scales", align_bytes=64)
         nc.vector.tensor_copy(k_scales[:], scale_pool[:].indirect(slots[:]))
@@ -105,8 +103,18 @@ def tile_attend_gvaluestore_kernel(tc, query, keys_words, keys_scales, qs, grows
         k_codes = sb.tile([P, I], U32, name="k_codes", align_bytes=64)
         nc.vector.tensor_copy(k_codes[:], key_pool[:].indirect(slots[:]))
 
+        faded_lo0 = sb.tile([P, HALF], F32, name="faded_lo0")
+        nc.vector.tensor_tensor(out=faded_lo0[:], in0=old_lo0[:], in1=fade_rows[:, 0:HALF], op=ALU.mult)
+        faded_lo1 = sb.tile([P, HALF], F32, name="faded_lo1")
+        nc.gpsimd.tensor_tensor(out=faded_lo1[:], in0=old_lo1[:], in1=fade_rows[:, 0:HALF], op=ALU.mult)
+
         neg_max = sb.tile([P, PACK], F32, name="neg_max", tag="relay_a", align_bytes=64)
-        row_sum = sb.tile([P, PACK], F32, name="row_sum", tag="relay_b", align_bytes=64)
+        sums_early = sb.tile([P, PACK - 1], F32, name="sums_early", tag="relay_b", align_bytes=64)
+        sum_last = sb.tile([P, 1], F32, name="sum_last", tag="relay_c", align_bytes=64)
+
+        def row_sum(lo, hi):
+            return sum_last[:] if lo == PACK - 1 else sums_early[:, lo:hi]
+
         inv_sum = sb.tile([P, PACK], F32, name="inv_sum")
         probs = sb.tile([P, PACK, I], F32, name="probs")
         w_planes = sb.tile([P, PACK, I], BF16, name="w_planes")
@@ -124,11 +132,11 @@ def tile_attend_gvaluestore_kernel(tc, query, keys_words, keys_scales, qs, grows
             )
             nc.vector.tensor_reduce(out=neg_max[:, r : r + 1], in_=scores[:], axis=mybir.AxisListType.X, op=ALU.max, negate=True)
             nc.scalar.activation(
-                out=probs[:, r, :], in_=scores[:], func=ACT.Exp, bias=neg_max[:, r : r + 1], accum_out=row_sum[:, r : r + 1]
+                out=probs[:, r, :], in_=scores[:], func=ACT.Exp, bias=neg_max[:, r : r + 1], accum_out=row_sum(r, r + 1)
             )
 
         def invert(lo, hi):
-            nc.vector.reciprocal(inv_sum[:, lo:hi], row_sum[:, lo:hi])
+            nc.vector.reciprocal(inv_sum[:, lo:hi], row_sum(lo, hi))
 
         def weigh(r, lo, hi):
             nc.vector.tensor_scalar(
@@ -142,16 +150,6 @@ def tile_attend_gvaluestore_kernel(tc, query, keys_words, keys_scales, qs, grows
 
         g_codes = sb.tile([P, E], U32, name="g_codes", align_bytes=64)
         g_scales = sb.tile([P, E], U8, name="g_scales", align_bytes=64)
-        g_late = sb.tile([P, 2 * P * PACK], BF16, name="g_late", align_bytes=64)
-        for n in range(2):
-            nc.gpsimd.tensor_scalar(
-                out=g_late[:, n * P * PACK : (n + 1) * P * PACK].rearrange("p (e j) -> p e j", j=PACK),
-                in0=g_raw_hi[:, :, n * P : (n + 1) * P].rearrange("p j e -> p e j"),
-                scalar1=1.0,
-                scalar2=0.0,
-                op0=ALU.mult,
-                op1=ALU.add,
-            )
 
         def quantize_g(lo, hi, rounded):
             cols = slice(lo * P, hi * P)
@@ -165,16 +163,22 @@ def tile_attend_gvaluestore_kernel(tc, query, keys_words, keys_scales, qs, grows
         weigh(2, 0, I)
         weigh(3, 0, P)
 
+        def round_g(rounded, m):
+            nc.scalar.copy(
+                rounded.rearrange("p (c n j) -> p c j n", n=4, j=PACK),
+                g_raw[:, :, m * P : (m + 1) * P].rearrange("p j (c n) -> p c j n", n=4),
+            )
+
         g_early = []
         for m, tag in enumerate(("relay_a", "relay_b")):
             t = sb.tile([P, P * PACK], BF16, name="g_early%d" % m, tag=tag, align_bytes=64)
-            nc.scalar.copy(
-                t[:].rearrange("p (c n j) -> p c j n", n=4, j=PACK),
-                g_raw_lo[:, :, m * P : (m + 1) * P].rearrange("p j (c n) -> p c j n", n=4),
-            )
+            round_g(t[:], m)
             g_early.append(t)
+        g_late = sb.tile([P, 2 * P * PACK], BF16, name="g_late", tag="relay_c", align_bytes=64)
+        for n in range(2):
+            round_g(g_late[:, n * P * PACK : (n + 1) * P * PACK], 2 + n)
 
-        w_bf = sb.tile([P, I * PACK], BF16, name="w_bf", tag="relay_c", align_bytes=64)
+        w_bf = sb.tile([P, I * PACK], BF16, name="w_bf", align_bytes=64)
         w_codes = sb.tile([P, I], U32, name="w_codes", align_bytes=64)
         w_scales = sb.tile([P, I], U8, name="w_scales", align_bytes=64)
 
@@ -193,10 +197,10 @@ def tile_attend_gvaluestore_kernel(tc, query, keys_words, keys_scales, qs, grows
         weave(0, P, nc.vector.tensor_copy)
         weigh(3, P, I)
         quantize_w(0, P)
-        weave(P, I, nc.scalar.copy)
-        quantize_g(2, 4, g_late)
+        weave(P, I, nc.vector.tensor_copy)
         quantize_g(1, 2, g_early[1])
         quantize_w(P, I)
+        quantize_g(2, 4, g_late)
 
         dv = {}
 
@@ -238,27 +242,19 @@ def tile_attend_gvaluestore_kernel(tc, query, keys_words, keys_scales, qs, grows
         fade_turned(3)
         value_gradient(3, 0, I, 6, nc.scalar.copy)
         faded_hi = {}
-        for n, m in enumerate((0, 2, 1, 3)):
+        for n, m in enumerate((0, 1, 2, 3)):
             back = bank((4 + n) % 6, [P, HALF_BLOCKS, P], "faded_hi%d" % m)
             for b in range(HALF_BLOCKS):
                 nc.tensor.transpose(back[:, b, :], faded_t[b][:, m * P : (m + 1) * P], ident[:])
             faded_hi[m] = back
 
-        faded_lo = sb.tile([P, E_TILES, HALF], F32, name="faded_lo", tag="relay_c", align_bytes=64)
+        faded_lo23 = sb.tile([P, 2, HALF], F32, name="faded_lo23", tag="relay_c", align_bytes=64)
+        faded_lo = [faded_lo0[:], faded_lo1[:], faded_lo23[:, 0, :], faded_lo23[:, 1, :]]
         fade_lo = fade_rows[:, 0:HALF].rearrange("p (o u) -> p o u", o=1)
 
-        def fade_low(lo, hi):
-            nc.gpsimd.tensor_tensor(
-                out=faded_lo[:, lo:hi, :],
-                in0=old_lo[lo // 2][:, lo % 2 : lo % 2 + hi - lo, :],
-                in1=fade_lo.to_broadcast([P, hi - lo, HALF]),
-                op=ALU.mult,
-            )
-
-        def finish_low(m, engine, lo, hi):
-            y = sb.tile([P, hi - lo], F32, name="y_lo%d_%d" % (m, lo))
-            engine.tensor_tensor(out=y[:], in0=faded_lo[:, m, lo:hi], in1=stores[m][:, lo:hi], op=ALU.add)
-            nc.sync.dma_start(out=out[m * P : (m + 1) * P, lo:hi], in_=y[:])
+        def finish_low(m, y):
+            nc.gpsimd.tensor_tensor(out=y, in0=faded_lo[m], in1=stores[m][:, 0:HALF], op=ALU.add)
+            nc.sync.dma_start(out=out[m * P : (m + 1) * P, 0:HALF], in_=y)
 
         def finish_high(m):
             y = sb.tile([P, HALF], F32, name="y_hi%d" % m)
@@ -274,14 +270,14 @@ def tile_attend_gvaluestore_kernel(tc, query, keys_words, keys_scales, qs, grows
         scatter(1, 0, I)
         scatter(0, P, I)
         scatter(2, 0, I)
-        fade_low(0, 2)
-        fade_low(2, 4)
-        finish_low(1, nc.gpsimd, 0, HALF)
-        finish_low(0, nc.gpsimd, 0, HALF)
-        finish_low(2, nc.gpsimd, 0, HALF)
-        for m in (0, 2, 1):
-            finish_high(m)
+        nc.gpsimd.tensor_tensor(out=faded_lo23[:], in0=old_lo23[:], in1=fade_lo.to_broadcast([P, 2, HALF]), op=ALU.mult)
+        y_lo01 = sb.tile([P, 2, HALF], F32, name="y_lo01", tag="relay_d")
+        y_lo23 = sb.tile([P, 2, HALF], F32, name="y_lo23")
+        finish_low(1, y_lo01[:, 1, :])
+        finish_low(0, y_lo01[:, 0, :])
+        finish_low(2, y_lo23[:, 0, :])
+        finish_high(0)
         scatter(3, 0, I)
-        finish_low(3, nc.gpsimd, 0, HALF // 2)
-        finish_high(3)
-        finish_low(3, nc.vector, HALF // 2, HALF)
+        finish_low(3, y_lo23[:, 1, :])
+        for m in range(1, E_TILES):
+            finish_high(m)

@@ -23,7 +23,6 @@ HALF = U // 2
 HALF_BLOCKS = HALF // P
 QUERY_SPLIT = 80
 RUN = U // P
-WINDOWS = 3
 
 
 def tile_attend_gvaluestore_kernel(tc, query, keys_words, keys_scales, qs, grows, old, fade, offs, offs2, out):
@@ -67,12 +66,11 @@ def tile_attend_gvaluestore_kernel(tc, query, keys_words, keys_scales, qs, grows
 
         ident = sb.tile([P, P], F32, name="ident")
         make_identity(nc, ident[:])
-        windows = []
-        for n in range(WINDOWS):
-            t = sb.tile([P, U], F32, name="window%d" % n)
-            (nc.gpsimd if n == WINDOWS - 1 else nc.vector).memset(t[:], 0.0)
-            windows.append(t)
-        stores = windows + [windows[0]]
+        stores = []
+        for m in range(E_TILES):
+            t = sb.tile([P, U], F32, name="window%d" % m)
+            (nc.gpsimd if m == E_TILES - 1 else nc.vector).memset(t[:], 0.0)
+            stores.append(t)
 
         k_scales = sb.tile([P, I], U8, name="k_scales", align_bytes=64)
         nc.vector.tensor_copy(k_scales[:], scale_pool[:].indirect(slots[:]))
@@ -234,13 +232,11 @@ def tile_attend_gvaluestore_kernel(tc, query, keys_words, keys_scales, qs, grows
 
         value_gradient(0, 0, P, 6, nc.scalar.copy)
         value_gradient(1, 0, I, 7, nc.scalar.copy)
-        value_gradient(0, P, I, 6, nc.scalar.copy)
-        fade_turned(0)
-        fade_turned(1)
-        value_gradient(2, 0, I, 7, nc.scalar.copy)
-        fade_turned(2)
-        fade_turned(3)
+        value_gradient(0, P, I, 4, nc.scalar.copy)
+        value_gradient(2, 0, I, 5, nc.scalar.copy)
         value_gradient(3, 0, I, 6, nc.scalar.copy)
+        for b in range(HALF_BLOCKS):
+            fade_turned(b)
         faded_hi = {}
         for n, m in enumerate((0, 1, 2, 3)):
             back = bank((4 + n) % 6, [P, HALF_BLOCKS, P], "faded_hi%d" % m)
@@ -270,14 +266,13 @@ def tile_attend_gvaluestore_kernel(tc, query, keys_words, keys_scales, qs, grows
         scatter(1, 0, I)
         scatter(0, P, I)
         scatter(2, 0, I)
+        scatter(3, 0, I)
         nc.gpsimd.tensor_tensor(out=faded_lo23[:], in0=old_lo23[:], in1=fade_lo.to_broadcast([P, 2, HALF]), op=ALU.mult)
         y_lo01 = sb.tile([P, 2, HALF], F32, name="y_lo01", tag="relay_d")
         y_lo23 = sb.tile([P, 2, HALF], F32, name="y_lo23")
         finish_low(1, y_lo01[:, 1, :])
         finish_low(0, y_lo01[:, 0, :])
         finish_low(2, y_lo23[:, 0, :])
-        finish_high(0)
-        scatter(3, 0, I)
         finish_low(3, y_lo23[:, 1, :])
-        for m in range(1, E_TILES):
+        for m in range(E_TILES):
             finish_high(m)

from contextlib import ExitStack

import concourse.mybir as mybir
from concourse.masks import make_identity

D, E, T, I, U, Q = 512, 512, 2048, 256, 1024, 512
FLOPS = 2 * D * Q * I + 2 * Q * E * I

F32 = mybir.dt.float32
BF16 = mybir.dt.bfloat16
I32 = mybir.dt.int32
U32 = mybir.dt.uint32
U16 = mybir.dt.uint16
U8 = mybir.dt.uint8
FP8X4 = mybir.dt.float8_e4m3fn_x4
ALU = mybir.AluOpType
ACT = mybir.ActivationFunctionType

P = 128
PACK = 4
E_TILES = E // P
HALF = U // 2
HALF_BLOCKS = HALF // P
QUERY_SPLIT = 80
RUN = U // P


def tile_attend_gvaluestore_kernel(tc, query, keys_words, keys_scales, qs, grows, old, fade, offs, offs2, out):
    nc = tc.nc
    with ExitStack() as ctx:
        sb = ctx.enter_context(tc.tile_pool(name="sb", bufs=1))
        ps = ctx.enter_context(tc.psum_pool(name="ps", bufs=1))

        def bank(n, shape, name):
            return ps.tile(shape, F32, name=name, tag="bank%d" % n)

        scale_pool = sb.tile([P, T], U8, name="scale_pool")
        nc.vector.memset(scale_pool[:].bitcast(I32), 0)
        slots = sb.tile([P, I // 16], U16, name="slots")
        nc.sync.dma_start(slots[:], offs)
        places = sb.tile([P, I // 16], U16, name="places")
        nc.sync.dma_start(places[:], offs2)
        q_raw = sb.tile([P, PACK, Q], F32, name="q_raw")
        nc.sync.dma_start(out=q_raw[:], in_=query.rearrange("(p j) q -> p j q", j=PACK))
        row_scale = sb.tile([P, PACK], F32, name="row_scale")
        nc.sync.dma_start(out=row_scale[:], in_=qs.rearrange("(p r) o -> p (r o)", r=PACK))
        fade_runs = sb.tile([P, RUN], F32, name="fade_runs")
        nc.sync.dma_start(out=fade_runs[:], in_=fade.rearrange("o (p c) -> (o p) c", c=RUN))
        for row in range(4):
            nc.sync.dma_start(
                out=scale_pool[row:P:32, :].bitcast(I32), in_=keys_scales[0, row:16:4, :].bitcast(I32)
            )
        key_pool = sb.tile([P, T], U32, name="key_pool")
        nc.sync.dma_start(out=key_pool[:].bitcast(I32), in_=keys_words[0].rearrange("p t r -> p (t r)").bitcast(I32))
        old_tiles = old.rearrange("(m p) u -> p m u", p=P)
        old_lo0 = sb.tile([P, HALF], F32, name="old_lo0", tag="relay_a", align_bytes=64)
        nc.sync.dma_start(out=old_lo0[:], in_=old_tiles[:, 0, 0:HALF])
        old_lo1 = sb.tile([P, HALF], F32, name="old_lo1")
        nc.sync.dma_start(out=old_lo1[:], in_=old_tiles[:, 1, 0:HALF])
        g_raw = sb.tile([P, PACK, E], F32, name="g_raw")
        nc.sync.dma_start(out=g_raw[:], in_=grows.rearrange("(p j) e -> p j e", j=PACK))
        old_hi = sb.tile([P, E_TILES, HALF], F32, name="old_hi")
        nc.sync.dma_start(out=old_hi[:], in_=old_tiles[:, :, HALF:U])
        old_lo23 = sb.tile([P, 2, HALF], F32, name="old_lo23", tag="relay_d")
        nc.sync.dma_start(out=old_lo23[:], in_=old_tiles[:, 2:4, 0:HALF])

        ident = sb.tile([P, P], F32, name="ident")
        make_identity(nc, ident[:])
        stores = []
        for m in range(E_TILES):
            t = sb.tile([P, U], F32, name="window%d" % m)
            (nc.gpsimd if m == E_TILES - 1 else nc.vector).memset(t[:], 0.0)
            stores.append(t)

        k_scales = sb.tile([P, I], U8, name="k_scales", align_bytes=64)
        nc.vector.tensor_copy(k_scales[:], scale_pool[:].indirect(slots[:]))

        fade_rows = sb.tile([P, U], F32, name="fade_rows")
        fade_by_run = fade_rows[:].rearrange("p (n c) -> p n c", c=RUN)
        for h in range(2):
            spread = bank(6 + h, [P, 4, P], "spread%d" % h)
            for c in range(4):
                col = 4 * h + c
                nc.tensor.transpose(spread[:, c, :], fade_runs[:, col : col + 1].to_broadcast([P, P]), ident[:])
            nc.scalar.copy(fade_by_run[:, :, 4 * h : 4 * h + 4], spread[:].rearrange("p c n -> p n c"))
        fade_ps = bank(5, [P, HALF_BLOCKS, P], "fade_ps")
        for b in range(HALF_BLOCKS):
            nc.tensor.transpose(fade_ps[:, b, :], fade_rows[:, HALF + b * P : HALF + (b + 1) * P], ident[:])
        fade_cols = sb.tile([P, HALF_BLOCKS], F32, name="fade_cols")
        nc.scalar.copy(fade_cols[:], fade_ps[:, :, 0])

        q_bf = sb.tile([P, Q * PACK], BF16, name="q_bf", align_bytes=64)
        q_dst = q_bf[:].rearrange("p (r s j) -> p s j r", r=PACK, j=PACK)
        q_src = q_raw[:].rearrange("p j (s r) -> p s j r", r=PACK)
        nc.vector.tensor_copy(q_dst[:, 0:QUERY_SPLIT], q_src[:, 0:QUERY_SPLIT])
        nc.scalar.copy(q_dst[:, QUERY_SPLIT:P], q_src[:, QUERY_SPLIT:P])
        q_codes = sb.tile([P, Q], U32, name="q_codes", align_bytes=64)
        q_scales = sb.tile([P, Q], U8, name="q_scales", align_bytes=64)
        nc.vector.quantize_mx(out=q_codes[:].bitcast(FP8X4), scales=q_scales[:], in_=q_bf[:])

        k_codes = sb.tile([P, I], U32, name="k_codes", align_bytes=64)
        nc.vector.tensor_copy(k_codes[:], key_pool[:].indirect(slots[:]))

        faded_lo0 = sb.tile([P, HALF], F32, name="faded_lo0")
        nc.vector.tensor_tensor(out=faded_lo0[:], in0=old_lo0[:], in1=fade_rows[:, 0:HALF], op=ALU.mult)
        faded_lo1 = sb.tile([P, HALF], F32, name="faded_lo1")
        nc.gpsimd.tensor_tensor(out=faded_lo1[:], in0=old_lo1[:], in1=fade_rows[:, 0:HALF], op=ALU.mult)

        neg_max = sb.tile([P, PACK], F32, name="neg_max", tag="relay_a", align_bytes=64)
        sums_early = sb.tile([P, PACK - 1], F32, name="sums_early", tag="relay_b", align_bytes=64)
        sum_last = sb.tile([P, 1], F32, name="sum_last", tag="relay_c", align_bytes=64)

        def row_sum(lo, hi):
            return sum_last[:] if lo == PACK - 1 else sums_early[:, lo:hi]

        inv_sum = sb.tile([P, PACK], F32, name="inv_sum")
        probs = sb.tile([P, PACK, I], F32, name="probs")
        w_planes = sb.tile([P, PACK, I], BF16, name="w_planes")
        for r in range(PACK):
            scores = bank(r, [P, I], "scores%d" % r)
            cols = slice(r * P, (r + 1) * P)
            nc.tensor.matmul_mx(
                out=scores[:],
                lhsT=q_codes[:, cols].bitcast(FP8X4),
                lhsT_scale=q_scales[:, cols],
                rhs=k_codes[:].bitcast(FP8X4),
                rhs_scale=k_scales[:],
                start=True,
                stop=True,
            )
            nc.vector.tensor_reduce(out=neg_max[:, r : r + 1], in_=scores[:], axis=mybir.AxisListType.X, op=ALU.max, negate=True)
            nc.scalar.activation(
                out=probs[:, r, :], in_=scores[:], func=ACT.Exp, bias=neg_max[:, r : r + 1], accum_out=row_sum(r, r + 1)
            )

        def invert(lo, hi):
            nc.vector.reciprocal(inv_sum[:, lo:hi], row_sum(lo, hi))

        def weigh(r, lo, hi):
            nc.vector.tensor_scalar(
                out=w_planes[:, r, lo:hi],
                in0=probs[:, r, lo:hi],
                scalar1=inv_sum[:, r : r + 1],
                scalar2=row_scale[:, r : r + 1],
                op0=ALU.mult,
                op1=ALU.mult,
            )

        g_codes = sb.tile([P, E], U32, name="g_codes", align_bytes=64)
        g_scales = sb.tile([P, E], U8, name="g_scales", align_bytes=64)

        def quantize_g(lo, hi, rounded):
            cols = slice(lo * P, hi * P)
            nc.vector.quantize_mx(out=g_codes[:, cols].bitcast(FP8X4), scales=g_scales[:, cols], in_=rounded[:])

        invert(0, 2)
        invert(2, 3)
        weigh(0, 0, I)
        weigh(1, 0, I)
        invert(3, 4)
        weigh(2, 0, I)
        weigh(3, 0, P)

        def round_g(rounded, m):
            nc.scalar.copy(
                rounded.rearrange("p (c n j) -> p c j n", n=4, j=PACK),
                g_raw[:, :, m * P : (m + 1) * P].rearrange("p j (c n) -> p c j n", n=4),
            )

        g_early = []
        for m, tag in enumerate(("relay_a", "relay_b")):
            t = sb.tile([P, P * PACK], BF16, name="g_early%d" % m, tag=tag, align_bytes=64)
            round_g(t[:], m)
            g_early.append(t)
        g_late = sb.tile([P, 2 * P * PACK], BF16, name="g_late", tag="relay_c", align_bytes=64)
        for n in range(2):
            round_g(g_late[:, n * P * PACK : (n + 1) * P * PACK], 2 + n)

        w_bf = sb.tile([P, I * PACK], BF16, name="w_bf", align_bytes=64)
        w_codes = sb.tile([P, I], U32, name="w_codes", align_bytes=64)
        w_scales = sb.tile([P, I], U8, name="w_scales", align_bytes=64)

        def weave(lo, hi, copy):
            copy(
                w_bf[:, lo * PACK : hi * PACK].rearrange("p (c n r) -> p c r n", n=4, r=PACK),
                w_planes[:, :, lo:hi].rearrange("p r (c n) -> p c r n", n=4),
            )

        def quantize_w(lo, hi):
            nc.vector.quantize_mx(
                out=w_codes[:, lo:hi].bitcast(FP8X4), scales=w_scales[:, lo:hi], in_=w_bf[:, lo * PACK : hi * PACK]
            )

        quantize_g(0, 1, g_early[0])
        weave(0, P, nc.vector.tensor_copy)
        weigh(3, P, I)
        quantize_w(0, P)
        weave(P, I, nc.vector.tensor_copy)
        quantize_g(1, 2, g_early[1])
        quantize_w(P, I)
        quantize_g(2, 4, g_late)

        dv = {}

        def value_gradient(m, lo, hi, n, copy):
            acc = bank(n, [P, hi - lo], "dv_ps%d_%d" % (m, lo))
            cols = slice(m * P, (m + 1) * P)
            nc.tensor.matmul_mx(
                out=acc[:],
                lhsT=g_codes[:, cols].bitcast(FP8X4),
                lhsT_scale=g_scales[:, cols],
                rhs=w_codes[:, lo:hi].bitcast(FP8X4),
                rhs_scale=w_scales[:, lo:hi],
                start=True,
                stop=True,
            )
            t = sb.tile([P, hi - lo], F32, name="dv%d_%d" % (m, lo))
            copy(t[:], acc[:])
            dv[m, lo] = t

        faded_t = []

        def fade_turned(b):
            turned = bank(b, [P, E_TILES, P], "turned%d" % b)
            for m in range(E_TILES):
                nc.tensor.transpose(turned[:, m, :], old_hi[:, m, b * P : (b + 1) * P], ident[:])
            t = sb.tile([P, E], F32, name="faded_t%d" % b)
            nc.scalar.activation(
                out=t[:], in_=turned[:].rearrange("p m e -> p (m e)"), func=ACT.Copy, scale=fade_cols[:, b : b + 1]
            )
            faded_t.append(t)

        value_gradient(0, 0, P, 6, nc.scalar.copy)
        value_gradient(1, 0, I, 7, nc.scalar.copy)
        value_gradient(0, P, I, 4, nc.scalar.copy)
        value_gradient(2, 0, I, 5, nc.scalar.copy)
        value_gradient(3, 0, I, 6, nc.scalar.copy)
        for b in range(HALF_BLOCKS):
            fade_turned(b)
        faded_hi = {}
        for n, m in enumerate((0, 1, 2, 3)):
            back = bank((4 + n) % 6, [P, HALF_BLOCKS, P], "faded_hi%d" % m)
            for b in range(HALF_BLOCKS):
                nc.tensor.transpose(back[:, b, :], faded_t[b][:, m * P : (m + 1) * P], ident[:])
            faded_hi[m] = back

        faded_lo23 = sb.tile([P, 2, HALF], F32, name="faded_lo23", tag="relay_c", align_bytes=64)
        faded_lo = [faded_lo0[:], faded_lo1[:], faded_lo23[:, 0, :], faded_lo23[:, 1, :]]
        fade_lo = fade_rows[:, 0:HALF].rearrange("p (o u) -> p o u", o=1)

        def finish_low(m, y):
            nc.gpsimd.tensor_tensor(out=y, in0=faded_lo[m], in1=stores[m][:, 0:HALF], op=ALU.add)
            nc.sync.dma_start(out=out[m * P : (m + 1) * P, 0:HALF], in_=y)

        def finish_high(m):
            y = sb.tile([P, HALF], F32, name="y_hi%d" % m)
            nc.vector.tensor_tensor(
                out=y[:], in0=faded_hi[m][:].rearrange("p b c -> p (b c)"), in1=stores[m][:, HALF:U], op=ALU.add
            )
            nc.scalar.dma_start(out=out[m * P : (m + 1) * P, HALF:U], in_=y[:])

        def scatter(m, lo, hi):
            nc.vector.tensor_copy(stores[m][:].indirect(places[:, lo // 16 : hi // 16]), dv[m, lo][:])

        scatter(0, 0, P)
        scatter(1, 0, I)
        scatter(0, P, I)
        scatter(2, 0, I)
        scatter(3, 0, I)
        nc.gpsimd.tensor_tensor(out=faded_lo23[:], in0=old_lo23[:], in1=fade_lo.to_broadcast([P, 2, HALF]), op=ALU.mult)
        y_lo01 = sb.tile([P, 2, HALF], F32, name="y_lo01", tag="relay_d")
        y_lo23 = sb.tile([P, 2, HALF], F32, name="y_lo23")
        finish_low(1, y_lo01[:, 1, :])
        finish_low(0, y_lo01[:, 0, :])
        finish_low(2, y_lo23[:, 0, :])
        finish_low(3, y_lo23[:, 1, :])
        for m in range(E_TILES):
            finish_high(m)
